import numpy as np
import ml_dtypes


def mxq(x, axis, fmt="e4m3"):
    dtype, down = {"e4m3": (ml_dtypes.float8_e4m3fn, 7), "e5m2": (ml_dtypes.float8_e5m2, 14)}[fmt]
    v = np.moveaxis(np.asarray(x, np.float32).astype(ml_dtypes.bfloat16).astype(np.float64), axis, -1)
    blocks = v.reshape(v.shape[:-1] + (-1, 32))
    amax = np.abs(blocks).max(-1, keepdims=True)
    byte = np.maximum(np.where(amax > 0, np.frexp(amax)[1] - 1 + 127, 0) - down, 1)
    scale = np.exp2(byte - 127.0)
    codes = (blocks / scale).astype(np.float32).astype(dtype).astype(np.float64)
    return np.moveaxis((codes * scale).reshape(v.shape), -1, axis)


WIDE = False


def mx_kscale(k):
    if not WIDE:
        return np.ones(k)
    levels = np.array([10, -10, 5, -5, 0])
    if k % 512:
        return np.exp2(np.random.permutation(np.resize(levels, k // 32))).repeat(32)
    a = np.empty((k // 512, 16))
    for p in range(k // 512):
        a[p, :8] = np.random.permutation(np.resize(levels, 8))
        for g in range(8):
            far = levels[np.abs(levels - a[p, g]) >= 10]
            a[p, g + 8] = far[np.random.randint(len(far))]
    return np.exp2(a.ravel()).repeat(32)


def f64(x):
    return np.asarray(x).astype(np.float64)


def striped(idx):
    return np.tile(idx.reshape(-1, 16).T, (8, 1)).astype(np.uint16)


def unstriped(offs):
    return offs[:16].T.reshape(-1).astype(np.int64)


def pack_weight(w):
    k, n = w.shape
    w = f64(np.asarray(w, np.float32).astype(ml_dtypes.bfloat16)).reshape(k // 32, 32, n)
    amax = np.abs(w).max(1)
    byte = np.clip(np.where(amax > 0, np.frexp(amax)[1] - 1 + 127 - 7, 1), 1, 254)
    scaled = (w * np.exp2(127.0 - byte)[:, None, :]).reshape(k, n).astype(np.float32)
    words = np.ascontiguousarray(scaled.reshape(k // 512, 128, 4, n).transpose(0, 1, 3, 2)).astype(ml_dtypes.float8_e4m3fn).view(np.uint8)
    return words, np.ascontiguousarray(byte.astype(np.uint8).reshape(k // 512, 16, n))


def unpack_weight(words, scales):
    g, p, n, _ = words.shape
    vals = np.ascontiguousarray(words).view(ml_dtypes.float8_e4m3fn).astype(np.float64) * np.repeat(np.exp2(scales.astype(np.float64) - 127.0), 8, axis=1)[..., None]
    return vals.transpose(0, 1, 3, 2).reshape(g * 512, n)


def relu(v):
    return np.maximum(v, 0.0)


K, T, S, N, U = 512, 1024, 512, 256, 1024


def setup_inputs():
    n = np.random.standard_normal
    s = mx_kscale(K)[:, None]
    packed_xT = pack_weight(n((K, T)) * s)
    return {
        "x_words": packed_xT[0],
        "x_scales": packed_xT[1],
        "w1": (n((K, N)) / np.sqrt(K) / s).astype(np.float32),
        "var": (np.random.uniform(0.3, 2.0, (N, U))).astype(np.float32),
        "omega": (np.random.uniform(0.02, 0.15, (N, 1))).astype(np.float32),
        "ret": (n((N, S))).astype(np.float32),
        "offs": striped(np.random.permutation(T)[:S]),
        "ser": striped(np.random.permutation(U)[:S]),
    }


def reference(x_words, x_scales, w1, var, omega, ret, offs, ser):
    v0 = f64(var)[:, unstriped(ser)]
    xq = unpack_weight(x_words, x_scales)[:, unstriped(offs)]
    y = mxq(f64(w1), 0, "e4m3").T @ xq
    shk = (0.9 * y) * np.sqrt(v0)
    v1 = 0.8 * v0 + f64(omega) + 0.08 * ((shk) ** 2) + 0.12 * ((relu(-1.0 * shk)) ** 2)
    return 0.5 * (np.log(v1) + ((f64(ret)) ** 2) / v1)

@@ -1,0 +1,123 @@
+import math
+from contextlib import ExitStack
+
+import concourse.mybir as mybir
+
+K, T, S, N, U = 512, 1024, 512, 256, 1024
+FLOPS = 2 * K * S * N
+
+F32 = mybir.dt.float32
+BF16 = mybir.dt.bfloat16
+I32 = mybir.dt.int32
+U32 = mybir.dt.uint32
+U16 = mybir.dt.uint16
+U8 = mybir.dt.uint8
+FP8X4 = mybir.dt.float8_e4m3fn_x4
+ACT = mybir.ActivationFunctionType
+ALU = mybir.AluOpType
+
+P = 128
+PACK = 4
+TILES = N // P
+HALF = S // 2
+
+UP = 0.81 * 0.08
+DOWN = 0.81 * (0.08 + 0.12)
+SPREAD = (DOWN - UP) / 2
+CENTRE = (DOWN + UP) / 2 / SPREAD
+
+
+def tile_picked_ygjrg_nll_p_kernel(tc, x_words, x_scales, w1, var, omega, ret, offs, ser, out):
+    nc = tc.nc
+    with ExitStack() as ctx:
+        keep = ctx.enter_context(tc.tile_pool(name="keep", bufs=1))
+        psum = ctx.enter_context(tc.psum_pool(name="psum", bufs=1))
+
+        offs_sb = keep.tile([P, S // 16], U16, name="offs_sb")
+        ser_sb = keep.tile([P, S // 16], U16, name="ser_sb")
+        words_all = keep.tile([P, T], U32, name="words_all", align_bytes=64)
+        scales_all = keep.tile([P, T], U8, name="scales_all", align_bytes=64)
+        w_raw = keep.tile([P, PACK, N], F32, name="w_raw", align_bytes=64)
+        var_all = [keep.tile([P, U], F32, name="var_all%d" % h, align_bytes=64) for h in range(TILES)]
+        omega_sb = keep.tile([P, TILES], F32, name="omega_sb")
+        ret_sb = keep.tile([P, TILES, S], F32, name="ret_sb", align_bytes=64)
+
+        nc.vector.memset(scales_all[:].bitcast(I32), 0)
+        nc.sync.dma_start(offs_sb[:], offs)
+        nc.sync.dma_start(words_all[:].bitcast(I32), x_words[0].rearrange("p n t -> p (n t)").bitcast(I32))
+        nc.sync.dma_start(ser_sb[:], ser)
+        for q in range(4):
+            nc.sync.dma_start(scales_all[32 * q : 32 * q + 4, :].bitcast(I32), x_scales[0, 4 * q : 4 * q + 4, :].bitcast(I32))
+        nc.sync.dma_start(w_raw[:], w1.rearrange("(p j) n -> p j n", j=PACK))
+        for h in range(TILES):
+            nc.sync.dma_start(var_all[h][:], var[h * P : (h + 1) * P, :])
+        with nc.allow_non_contiguous_dma(reason="one value a row"):
+            nc.sync.dma_start(omega_sb[:], omega.rearrange("(h p) o -> p (h o)", p=P))
+        nc.sync.dma_start(ret_sb[:], ret.rearrange("(h p) s -> p h s", p=P))
+
+        warm_in = keep.tile([P, 1], F32, name="warm_in")
+        warm_out = keep.tile([P, 1], F32, name="warm_out")
+        nc.gpsimd.memset(warm_in[:], 1.0)
+        nc.scalar.activation(warm_out[:], warm_in[:], ACT.Abs_reciprocal_sqrt)
+
+        x_scale = keep.tile([P, S], U8, name="x_scale", align_bytes=64)
+        x_code = keep.tile([P, S], U32, name="x_code", align_bytes=64)
+        nc.vector.tensor_copy(x_code[:], words_all[:].indirect(offs_sb[:]))
+        nc.vector.tensor_copy(x_scale[:], scales_all[:].indirect(offs_sb[:]))
+
+        v0 = []
+        y = []
+        for h in range(TILES):
+            w_bf = keep.tile([P, P, PACK], BF16, name="w_bf%d" % h, tag="stage%d" % h, align_bytes=64)
+            nc.scalar.copy(
+                w_bf[:].rearrange("p (c i) j -> p c j i", i=4),
+                w_raw[:, :, h * P : (h + 1) * P].rearrange("p j (c i) -> p c j i", i=4),
+            )
+            w_code = keep.tile([P, P], U32, name="w_code%d" % h, align_bytes=64)
+            w_scale = keep.tile([P, P], U8, name="w_scale%d" % h, align_bytes=64)
+            nc.vector.quantize_mx(out=w_code[:].bitcast(FP8X4), scales=w_scale[:], in_=w_bf[:].rearrange("p c j -> p (c j)"))
+            acc = psum.tile([P, S], F32, name="y%d" % h)
+            nc.tensor.matmul_mx(
+                out=acc[:],
+                lhsT=w_code[:].bitcast(FP8X4),
+                lhsT_scale=w_scale[:],
+                rhs=x_code[:].bitcast(FP8X4),
+                rhs_scale=x_scale[:],
+                start=True,
+                stop=True,
+            )
+            y.append(acc)
+        for h in range(TILES):
+            picked = keep.tile([P, S], F32, name="v0_%d" % h, tag="stage%d" % (TILES - 1 - h), align_bytes=64)
+            nc.vector.tensor_copy(picked[:], var_all[h][:].indirect(ser_sb[:]))
+            v0.append(picked)
+
+        sgn = keep.tile([P, TILES, S], F32, name="sgn", align_bytes=64)
+        sq = keep.tile([P, TILES, S], F32, name="sq", align_bytes=64)
+        shock = keep.tile([P, TILES, S], F32, name="shock", tag="chain", align_bytes=64)
+        carried = keep.tile([P, TILES, S], F32, name="carried", tag="reused", align_bytes=64)
+        z = keep.tile([P, TILES, S], F32, name="z", align_bytes=64)
+        for h in range(TILES):
+            nc.scalar.activation(sgn[:, h, :], y[h][:], ACT.Sign)
+            nc.scalar.activation(sq[:, h, :], y[h][:], ACT.Square, scale=math.sqrt(SPREAD))
+        for h in range(TILES):
+            nc.vector.scalar_tensor_tensor(shock[:, h, :], sgn[:, h, :], CENTRE, sq[:, h, :], ALU.subtract, ALU.mult)
+        for h, cols in ((0, slice(0, S)), (1, slice(0, HALF)), (1, slice(HALF, S))):
+            nc.vector.scalar_tensor_tensor(carried[:, h, cols], shock[:, h, cols], 0.8, v0[h][:, cols], ALU.subtract, ALU.mult)
+            nc.scalar.activation(z[:, h, cols], carried[:, h, cols], ACT.Abs_reciprocal_sqrt, scale=-1.0, bias=omega_sb[:, h : h + 1])
+
+        scaled = keep.tile([P, TILES, S], F32, name="scaled", tag="chain", align_bytes=64)
+        misfit = keep.tile([P, TILES, S], F32, name="misfit", align_bytes=64)
+        for h in range(TILES):
+            nc.vector.tensor_tensor(scaled[:, h, :], ret_sb[:, h, :], z[:, h, :], ALU.mult)
+        for h in range(TILES):
+            nc.vector.scalar_tensor_tensor(misfit[:, h, :], scaled[:, h, :], 0.5, scaled[:, h, :], ALU.mult, ALU.mult)
+
+        log_z = keep.tile([P, TILES, S], F32, name="log_z", tag="reused", align_bytes=64)
+        res = keep.tile([P, TILES, S], F32, name="res", align_bytes=64)
+        for h in range(TILES):
+            for c0 in range(0, S, HALF):
+                cols = slice(c0, c0 + HALF)
+                nc.scalar.activation(log_z[:, h, cols], z[:, h, cols], ACT.Ln)
+                nc.vector.tensor_tensor(res[:, h, cols], misfit[:, h, cols], log_z[:, h, cols], ALU.subtract)
+                nc.sync.dma_start(out[h * P : (h + 1) * P, cols], res[:, h, cols])

@@ -65,10 +65,9 @@ def tile_picked_ygjrg_nll_p_kernel(tc, x_words, x_scales, w1, var, omega, ret, o
         nc.vector.tensor_copy(x_code[:], words_all[:].indirect(offs_sb[:]))
         nc.vector.tensor_copy(x_scale[:], scales_all[:].indirect(offs_sb[:]))
 
-        v0 = []
         y = []
         for h in range(TILES):
-            w_bf = keep.tile([P, P, PACK], BF16, name="w_bf%d" % h, tag="stage%d" % h, align_bytes=64)
+            w_bf = keep.tile([P, P, PACK], BF16, name="w_bf%d" % h, align_bytes=64)
             nc.scalar.copy(
                 w_bf[:].rearrange("p (c i) j -> p c j i", i=4),
                 w_raw[:, :, h * P : (h + 1) * P].rearrange("p j (c i) -> p c j i", i=4),
@@ -76,48 +75,54 @@ def tile_picked_ygjrg_nll_p_kernel(tc, x_words, x_scales, w1, var, omega, ret, o
             w_code = keep.tile([P, P], U32, name="w_code%d" % h, align_bytes=64)
             w_scale = keep.tile([P, P], U8, name="w_scale%d" % h, align_bytes=64)
             nc.vector.quantize_mx(out=w_code[:].bitcast(FP8X4), scales=w_scale[:], in_=w_bf[:].rearrange("p c j -> p (c j)"))
-            acc = psum.tile([P, S], F32, name="y%d" % h)
-            nc.tensor.matmul_mx(
-                out=acc[:],
-                lhsT=w_code[:].bitcast(FP8X4),
-                lhsT_scale=w_scale[:],
-                rhs=x_code[:].bitcast(FP8X4),
-                rhs_scale=x_scale[:],
-                start=True,
-                stop=True,
-            )
-            y.append(acc)
-        for h in range(TILES):
-            picked = keep.tile([P, S], F32, name="v0_%d" % h, tag="stage%d" % (TILES - 1 - h), align_bytes=64)
-            nc.vector.tensor_copy(picked[:], var_all[h][:].indirect(ser_sb[:]))
-            v0.append(picked)
-
-        sgn = keep.tile([P, TILES, S], F32, name="sgn", align_bytes=64)
-        sq = keep.tile([P, TILES, S], F32, name="sq", align_bytes=64)
-        shock = keep.tile([P, TILES, S], F32, name="shock", tag="chain", align_bytes=64)
-        carried = keep.tile([P, TILES, S], F32, name="carried", tag="reused", align_bytes=64)
-        z = keep.tile([P, TILES, S], F32, name="z", align_bytes=64)
-        for h in range(TILES):
-            nc.scalar.activation(sgn[:, h, :], y[h][:], ACT.Sign)
-            nc.scalar.activation(sq[:, h, :], y[h][:], ACT.Square, scale=math.sqrt(SPREAD))
-        for h in range(TILES):
-            nc.vector.scalar_tensor_tensor(shock[:, h, :], sgn[:, h, :], CENTRE, sq[:, h, :], ALU.subtract, ALU.mult)
-        for h, cols in ((0, slice(0, S)), (1, slice(0, HALF)), (1, slice(HALF, S))):
-            nc.vector.scalar_tensor_tensor(carried[:, h, cols], shock[:, h, cols], 0.8, v0[h][:, cols], ALU.subtract, ALU.mult)
-            nc.scalar.activation(z[:, h, cols], carried[:, h, cols], ACT.Abs_reciprocal_sqrt, scale=-1.0, bias=omega_sb[:, h : h + 1])
-
-        scaled = keep.tile([P, TILES, S], F32, name="scaled", tag="chain", align_bytes=64)
-        misfit = keep.tile([P, TILES, S], F32, name="misfit", align_bytes=64)
-        for h in range(TILES):
-            nc.vector.tensor_tensor(scaled[:, h, :], ret_sb[:, h, :], z[:, h, :], ALU.mult)
-        for h in range(TILES):
-            nc.vector.scalar_tensor_tensor(misfit[:, h, :], scaled[:, h, :], 0.5, scaled[:, h, :], ALU.mult, ALU.mult)
-
-        log_z = keep.tile([P, TILES, S], F32, name="log_z", tag="reused", align_bytes=64)
-        res = keep.tile([P, TILES, S], F32, name="res", align_bytes=64)
-        for h in range(TILES):
             for c0 in range(0, S, HALF):
-                cols = slice(c0, c0 + HALF)
-                nc.scalar.activation(log_z[:, h, cols], z[:, h, cols], ACT.Ln)
-                nc.vector.tensor_tensor(res[:, h, cols], misfit[:, h, cols], log_z[:, h, cols], ALU.subtract)
-                nc.sync.dma_start(out[h * P : (h + 1) * P, cols], res[:, h, cols])
+                acc = psum.tile([P, HALF], F32, name="y%d_%d" % (h, c0))
+                nc.tensor.matmul_mx(
+                    out=acc[:],
+                    lhsT=w_code[:].bitcast(FP8X4),
+                    lhsT_scale=w_scale[:],
+                    rhs=x_code[:, c0 : c0 + HALF].bitcast(FP8X4),
+                    rhs_scale=x_scale[:, c0 : c0 + HALF],
+                    start=True,
+                    stop=True,
+                )
+                y.append(acc)
+
+        def wide(name, tag=None):
+            return keep.tile([P, TILES * S], F32, name=name, tag=tag or name, align_bytes=64)
+
+        quarters = [slice(c0, c0 + HALF) for c0 in range(0, TILES * S, HALF)]
+        v0 = wide("v0")
+        for h in range(TILES):
+            nc.vector.tensor_copy(v0[:, h * S : (h + 1) * S], var_all[h][:].indirect(ser_sb[:]))
+
+        sgn = wide("sgn")
+        sq = wide("sq")
+        for cols, acc in zip(quarters, y):
+            nc.scalar.activation(sgn[:, cols], acc[:], ACT.Sign)
+            nc.scalar.activation(sq[:, cols], acc[:], ACT.Square, scale=math.sqrt(SPREAD))
+        shock = wide("shock", "shock_scaled")
+        for cols in (slice(0, 512), slice(512, 768), slice(768, 1024),):
+            nc.vector.scalar_tensor_tensor(shock[:, cols], sgn[:, cols], CENTRE, sq[:, cols], ALU.subtract, ALU.mult)
+        carried = wide("carried", "carried_log")
+        z = wide("z")
+        for cols in quarters:
+            h = cols.start // S
+            nc.vector.scalar_tensor_tensor(carried[:, cols], shock[:, cols], 0.8, v0[:, cols], ALU.subtract, ALU.mult)
+            nc.scalar.activation(z[:, cols], carried[:, cols], ACT.Abs_reciprocal_sqrt, scale=-1.0, bias=omega_sb[:, h : h + 1])
+
+        ret_flat = ret_sb[:].rearrange("p h s -> p (h s)")
+        scaled = wide("scaled", "shock_scaled")
+        misfit = wide("misfit")
+        for cols in (slice(0, 256), slice(256, 512), slice(512, 1024),):
+            nc.vector.tensor_tensor(scaled[:, cols], ret_flat[:, cols], z[:, cols], ALU.mult)
+        for cols in (slice(0, 256), slice(256, 512), slice(512, 1024),):
+            nc.vector.scalar_tensor_tensor(misfit[:, cols], scaled[:, cols], 0.5, scaled[:, cols], ALU.mult, ALU.mult)
+
+        log_z = wide("log_z", "carried_log")
+        res = wide("res")
+        for cols in (slice(0, 256), slice(256, 512), slice(512, 768), slice(768, 896), slice(896, 1024),):
+            h, c0 = divmod(cols.start, S)
+            nc.scalar.activation(log_z[:, cols], z[:, cols], ACT.Ln)
+            nc.vector.tensor_tensor(res[:, cols], misfit[:, cols], log_z[:, cols], ALU.subtract)
+            nc.sync.dma_start(out[h * P : (h + 1) * P, c0 : c0 + cols.stop - cols.start], res[:, cols])

@@ -18,13 +18,28 @@ ALU = mybir.AluOpType
 
 P = 128
 PACK = 4
+LINE = 4
 TILES = N // P
-HALF = S // 2
+QUARTER = S // 2
+EIGHTH = S // 4
 
-UP = 0.81 * 0.08
-DOWN = 0.81 * (0.08 + 0.12)
-SPREAD = (DOWN - UP) / 2
-CENTRE = (DOWN + UP) / 2 / SPREAD
+C_UP = 0.81 * 0.08
+C_DOWN = 0.81 * (0.08 + 0.12)
+SPREAD = (C_DOWN - C_UP) / 2
+CENTRE = (C_DOWN + C_UP) / 2 / SPREAD
+
+
+def steps(*widths):
+    starts = [sum(widths[:i]) for i in range(len(widths))]
+    return [slice(start, start + width) for start, width in zip(starts, widths)]
+
+
+MATMUL_STEPS = steps(*[QUARTER] * 4)
+SHOCK_STEPS = steps(S, QUARTER, QUARTER)
+VARIANCE_STEPS = steps(QUARTER, QUARTER, *[EIGHTH] * 4)
+MISFIT_STEPS = steps(QUARTER, QUARTER, S)
+LOG_STEPS = steps(*[EIGHTH] * 8)
+STORE_STEPS = steps(QUARTER, QUARTER, QUARTER, EIGHTH, EIGHTH)
 
 
 def tile_picked_ygjrg_nll_p_kernel(tc, x_words, x_scales, w1, var, omega, ret, offs, ser, out):
@@ -46,12 +61,15 @@ def tile_picked_ygjrg_nll_p_kernel(tc, x_words, x_scales, w1, var, omega, ret, o
         nc.sync.dma_start(offs_sb[:], offs)
         nc.sync.dma_start(words_all[:].bitcast(I32), x_words[0].rearrange("p n t -> p (n t)").bitcast(I32))
         nc.sync.dma_start(ser_sb[:], ser)
-        for q in range(4):
-            nc.sync.dma_start(scales_all[32 * q : 32 * q + 4, :].bitcast(I32), x_scales[0, 4 * q : 4 * q + 4, :].bitcast(I32))
+        for q in range(P // 32):
+            nc.sync.dma_start(
+                scales_all[32 * q : 32 * q + PACK, :].bitcast(I32),
+                x_scales[0, PACK * q : PACK * (q + 1), :].bitcast(I32),
+            )
         nc.sync.dma_start(w_raw[:], w1.rearrange("(p j) n -> p j n", j=PACK))
         for h in range(TILES):
             nc.sync.dma_start(var_all[h][:], var[h * P : (h + 1) * P, :])
-        with nc.allow_non_contiguous_dma(reason="one value a row"):
+        with nc.allow_non_contiguous_dma(reason="omega has one value a row"):
             nc.sync.dma_start(omega_sb[:], omega.rearrange("(h p) o -> p (h o)", p=P))
         nc.sync.dma_start(ret_sb[:], ret.rearrange("(h p) s -> p h s", p=P))
 
@@ -69,20 +87,20 @@ def tile_picked_ygjrg_nll_p_kernel(tc, x_words, x_scales, w1, var, omega, ret, o
         for h in range(TILES):
             w_bf = keep.tile([P, P, PACK], BF16, name="w_bf%d" % h, align_bytes=64)
             nc.scalar.copy(
-                w_bf[:].rearrange("p (c i) j -> p c j i", i=4),
-                w_raw[:, :, h * P : (h + 1) * P].rearrange("p j (c i) -> p c j i", i=4),
+                w_bf[:].rearrange("p (c i) j -> p c j i", i=LINE),
+                w_raw[:, :, h * P : (h + 1) * P].rearrange("p j (c i) -> p c j i", i=LINE),
             )
             w_code = keep.tile([P, P], U32, name="w_code%d" % h, align_bytes=64)
             w_scale = keep.tile([P, P], U8, name="w_scale%d" % h, align_bytes=64)
             nc.vector.quantize_mx(out=w_code[:].bitcast(FP8X4), scales=w_scale[:], in_=w_bf[:].rearrange("p c j -> p (c j)"))
-            for c0 in range(0, S, HALF):
-                acc = psum.tile([P, HALF], F32, name="y%d_%d" % (h, c0))
+            for j0 in range(0, S, QUARTER):
+                acc = psum.tile([P, QUARTER], F32, name="y%d_%d" % (h, j0))
                 nc.tensor.matmul_mx(
                     out=acc[:],
                     lhsT=w_code[:].bitcast(FP8X4),
                     lhsT_scale=w_scale[:],
-                    rhs=x_code[:, c0 : c0 + HALF].bitcast(FP8X4),
-                    rhs_scale=x_scale[:, c0 : c0 + HALF],
+                    rhs=x_code[:, j0 : j0 + QUARTER].bitcast(FP8X4),
+                    rhs_scale=x_scale[:, j0 : j0 + QUARTER],
                     start=True,
                     stop=True,
                 )
@@ -91,38 +109,39 @@ def tile_picked_ygjrg_nll_p_kernel(tc, x_words, x_scales, w1, var, omega, ret, o
         def wide(name, tag=None):
             return keep.tile([P, TILES * S], F32, name=name, tag=tag or name, align_bytes=64)
 
-        quarters = [slice(c0, c0 + HALF) for c0 in range(0, TILES * S, HALF)]
         v0 = wide("v0")
         for h in range(TILES):
             nc.vector.tensor_copy(v0[:, h * S : (h + 1) * S], var_all[h][:].indirect(ser_sb[:]))
 
         sgn = wide("sgn")
         sq = wide("sq")
-        for cols, acc in zip(quarters, y):
+        for cols, acc in zip(MATMUL_STEPS, y):
             nc.scalar.activation(sgn[:, cols], acc[:], ACT.Sign)
             nc.scalar.activation(sq[:, cols], acc[:], ACT.Square, scale=math.sqrt(SPREAD))
-        shock = wide("shock", "shock_scaled")
-        for cols in (slice(0, 512), slice(512, 768), slice(768, 1024),):
+        shock = wide("shock")
+        for cols in SHOCK_STEPS:
             nc.vector.scalar_tensor_tensor(shock[:, cols], sgn[:, cols], CENTRE, sq[:, cols], ALU.subtract, ALU.mult)
+
         carried = wide("carried", "carried_log")
         z = wide("z")
-        for cols in quarters:
+        for cols in VARIANCE_STEPS:
             h = cols.start // S
             nc.vector.scalar_tensor_tensor(carried[:, cols], shock[:, cols], 0.8, v0[:, cols], ALU.subtract, ALU.mult)
             nc.scalar.activation(z[:, cols], carried[:, cols], ACT.Abs_reciprocal_sqrt, scale=-1.0, bias=omega_sb[:, h : h + 1])
 
-        ret_flat = ret_sb[:].rearrange("p h s -> p (h s)")
-        scaled = wide("scaled", "shock_scaled")
+        ret_wide = ret_sb[:].rearrange("p h s -> p (h s)")
+        scaled = wide("scaled")
         misfit = wide("misfit")
-        for cols in (slice(0, 256), slice(256, 512), slice(512, 1024),):
-            nc.vector.tensor_tensor(scaled[:, cols], ret_flat[:, cols], z[:, cols], ALU.mult)
-        for cols in (slice(0, 256), slice(256, 512), slice(512, 1024),):
+        for cols in MISFIT_STEPS:
+            nc.vector.tensor_tensor(scaled[:, cols], ret_wide[:, cols], z[:, cols], ALU.mult)
+        for cols in MISFIT_STEPS:
             nc.vector.scalar_tensor_tensor(misfit[:, cols], scaled[:, cols], 0.5, scaled[:, cols], ALU.mult, ALU.mult)
 
         log_z = wide("log_z", "carried_log")
         res = wide("res")
-        for cols in (slice(0, 256), slice(256, 512), slice(512, 768), slice(768, 896), slice(896, 1024),):
-            h, c0 = divmod(cols.start, S)
+        for cols in LOG_STEPS:
             nc.scalar.activation(log_z[:, cols], z[:, cols], ACT.Ln)
             nc.vector.tensor_tensor(res[:, cols], misfit[:, cols], log_z[:, cols], ALU.subtract)
-            nc.sync.dma_start(out[h * P : (h + 1) * P, c0 : c0 + cols.stop - cols.start], res[:, cols])
+        for cols in STORE_STEPS:
+            h, j0 = divmod(cols.start, S)
+            nc.sync.dma_start(out[h * P : (h + 1) * P, j0 : j0 + cols.stop - cols.start], res[:, cols])

import math
from contextlib import ExitStack

import concourse.mybir as mybir

K, T, S, N, U = 512, 1024, 512, 256, 1024
FLOPS = 2 * K * S * N

F32 = mybir.dt.float32
BF16 = mybir.dt.bfloat16
I32 = mybir.dt.int32
U32 = mybir.dt.uint32
U16 = mybir.dt.uint16
U8 = mybir.dt.uint8
FP8X4 = mybir.dt.float8_e4m3fn_x4
ACT = mybir.ActivationFunctionType
ALU = mybir.AluOpType

P = 128
PACK = 4
LINE = 4
TILES = N // P
QUARTER = S // 2
EIGHTH = S // 4

C_UP = 0.81 * 0.08
C_DOWN = 0.81 * (0.08 + 0.12)
SPREAD = (C_DOWN - C_UP) / 2
CENTRE = (C_DOWN + C_UP) / 2 / SPREAD


def steps(*widths):
    starts = [sum(widths[:i]) for i in range(len(widths))]
    return [slice(start, start + width) for start, width in zip(starts, widths)]


MATMUL_STEPS = steps(*[QUARTER] * 4)
SHOCK_STEPS = steps(S, QUARTER, QUARTER)
VARIANCE_STEPS = steps(QUARTER, QUARTER, *[EIGHTH] * 4)
MISFIT_STEPS = steps(QUARTER, QUARTER, S)
LOG_STEPS = steps(*[EIGHTH] * 8)
STORE_STEPS = steps(QUARTER, QUARTER, QUARTER, EIGHTH, EIGHTH)


def tile_picked_ygjrg_nll_p_kernel(tc, x_words, x_scales, w1, var, omega, ret, offs, ser, out):
    nc = tc.nc
    with ExitStack() as ctx:
        keep = ctx.enter_context(tc.tile_pool(name="keep", bufs=1))
        psum = ctx.enter_context(tc.psum_pool(name="psum", bufs=1))

        offs_sb = keep.tile([P, S // 16], U16, name="offs_sb")
        ser_sb = keep.tile([P, S // 16], U16, name="ser_sb")
        words_all = keep.tile([P, T], U32, name="words_all", align_bytes=64)
        scales_all = keep.tile([P, T], U8, name="scales_all", align_bytes=64)
        w_raw = keep.tile([P, PACK, N], F32, name="w_raw", align_bytes=64)
        var_all = [keep.tile([P, U], F32, name="var_all%d" % h, align_bytes=64) for h in range(TILES)]
        omega_sb = keep.tile([P, TILES], F32, name="omega_sb")
        ret_sb = keep.tile([P, TILES, S], F32, name="ret_sb", align_bytes=64)

        nc.vector.memset(scales_all[:].bitcast(I32), 0)
        nc.sync.dma_start(offs_sb[:], offs)
        nc.sync.dma_start(words_all[:].bitcast(I32), x_words[0].rearrange("p n t -> p (n t)").bitcast(I32))
        nc.sync.dma_start(ser_sb[:], ser)
        for q in range(P // 32):
            nc.sync.dma_start(
                scales_all[32 * q : 32 * q + PACK, :].bitcast(I32),
                x_scales[0, PACK * q : PACK * (q + 1), :].bitcast(I32),
            )
        nc.sync.dma_start(w_raw[:], w1.rearrange("(p j) n -> p j n", j=PACK))
        for h in range(TILES):
            nc.sync.dma_start(var_all[h][:], var[h * P : (h + 1) * P, :])
        with nc.allow_non_contiguous_dma(reason="omega has one value a row"):
            nc.sync.dma_start(omega_sb[:], omega.rearrange("(h p) o -> p (h o)", p=P))
        nc.sync.dma_start(ret_sb[:], ret.rearrange("(h p) s -> p h s", p=P))

        warm_in = keep.tile([P, 1], F32, name="warm_in")
        warm_out = keep.tile([P, 1], F32, name="warm_out")
        nc.gpsimd.memset(warm_in[:], 1.0)
        nc.scalar.activation(warm_out[:], warm_in[:], ACT.Abs_reciprocal_sqrt)

        x_scale = keep.tile([P, S], U8, name="x_scale", align_bytes=64)
        x_code = keep.tile([P, S], U32, name="x_code", align_bytes=64)
        nc.vector.tensor_copy(x_code[:], words_all[:].indirect(offs_sb[:]))
        nc.vector.tensor_copy(x_scale[:], scales_all[:].indirect(offs_sb[:]))

        y = []
        for h in range(TILES):
            w_bf = keep.tile([P, P, PACK], BF16, name="w_bf%d" % h, align_bytes=64)
            nc.scalar.copy(
                w_bf[:].rearrange("p (c i) j -> p c j i", i=LINE),
                w_raw[:, :, h * P : (h + 1) * P].rearrange("p j (c i) -> p c j i", i=LINE),
            )
            w_code = keep.tile([P, P], U32, name="w_code%d" % h, align_bytes=64)
            w_scale = keep.tile([P, P], U8, name="w_scale%d" % h, align_bytes=64)
            nc.vector.quantize_mx(out=w_code[:].bitcast(FP8X4), scales=w_scale[:], in_=w_bf[:].rearrange("p c j -> p (c j)"))
            for j0 in range(0, S, QUARTER):
                acc = psum.tile([P, QUARTER], F32, name="y%d_%d" % (h, j0))
                nc.tensor.matmul_mx(
                    out=acc[:],
                    lhsT=w_code[:].bitcast(FP8X4),
                    lhsT_scale=w_scale[:],
                    rhs=x_code[:, j0 : j0 + QUARTER].bitcast(FP8X4),
                    rhs_scale=x_scale[:, j0 : j0 + QUARTER],
                    start=True,
                    stop=True,
                )
                y.append(acc)

        def wide(name, tag=None):
            return keep.tile([P, TILES * S], F32, name=name, tag=tag or name, align_bytes=64)

        v0 = wide("v0")
        for h in range(TILES):
            nc.vector.tensor_copy(v0[:, h * S : (h + 1) * S], var_all[h][:].indirect(ser_sb[:]))

        sgn = wide("sgn")
        sq = wide("sq")
        for cols, acc in zip(MATMUL_STEPS, y):
            nc.scalar.activation(sgn[:, cols], acc[:], ACT.Sign)
            nc.scalar.activation(sq[:, cols], acc[:], ACT.Square, scale=math.sqrt(SPREAD))
        shock = wide("shock")
        for cols in SHOCK_STEPS:
            nc.vector.scalar_tensor_tensor(shock[:, cols], sgn[:, cols], CENTRE, sq[:, cols], ALU.subtract, ALU.mult)

        carried = wide("carried", "carried_log")
        z = wide("z")
        for cols in VARIANCE_STEPS:
            h = cols.start // S
            nc.vector.scalar_tensor_tensor(carried[:, cols], shock[:, cols], 0.8, v0[:, cols], ALU.subtract, ALU.mult)
            nc.scalar.activation(z[:, cols], carried[:, cols], ACT.Abs_reciprocal_sqrt, scale=-1.0, bias=omega_sb[:, h : h + 1])

        ret_wide = ret_sb[:].rearrange("p h s -> p (h s)")
        scaled = wide("scaled")
        misfit = wide("misfit")
        for cols in MISFIT_STEPS:
            nc.vector.tensor_tensor(scaled[:, cols], ret_wide[:, cols], z[:, cols], ALU.mult)
        for cols in MISFIT_STEPS:
            nc.vector.scalar_tensor_tensor(misfit[:, cols], scaled[:, cols], 0.5, scaled[:, cols], ALU.mult, ALU.mult)

        log_z = wide("log_z", "carried_log")
        res = wide("res")
        for cols in LOG_STEPS:
            nc.scalar.activation(log_z[:, cols], z[:, cols], ACT.Ln)
            nc.vector.tensor_tensor(res[:, cols], misfit[:, cols], log_z[:, cols], ALU.subtract)
        for cols in STORE_STEPS:
            h, j0 = divmod(cols.start, S)
            nc.sync.dma_start(out[h * P : (h + 1) * P, j0 : j0 + cols.stop - cols.start], res[:, cols])
